import numpy as np
import ml_dtypes


def mxq(x, axis, fmt="e4m3"):
    dtype, down = {"e4m3": (ml_dtypes.float8_e4m3fn, 7), "e5m2": (ml_dtypes.float8_e5m2, 14)}[fmt]
    v = np.moveaxis(np.asarray(x, np.float32).astype(ml_dtypes.bfloat16).astype(np.float64), axis, -1)
    blocks = v.reshape(v.shape[:-1] + (-1, 32))
    amax = np.abs(blocks).max(-1, keepdims=True)
    byte = np.maximum(np.where(amax > 0, np.frexp(amax)[1] - 1 + 127, 0) - down, 1)
    scale = np.exp2(byte - 127.0)
    codes = (blocks / scale).astype(np.float32).astype(dtype).astype(np.float64)
    return np.moveaxis((codes * scale).reshape(v.shape), -1, axis)


WIDE = False


def mx_kscale(k):
    if not WIDE:
        return np.ones(k)
    levels = np.array([10, -10, 5, -5, 0])
    if k % 512:
        return np.exp2(np.random.permutation(np.resize(levels, k // 32))).repeat(32)
    a = np.empty((k // 512, 16))
    for p in range(k // 512):
        a[p, :8] = np.random.permutation(np.resize(levels, 8))
        for g in range(8):
            far = levels[np.abs(levels - a[p, g]) >= 10]
            a[p, g + 8] = far[np.random.randint(len(far))]
    return np.exp2(a.ravel()).repeat(32)


def f64(x):
    return np.asarray(x).astype(np.float64)


def striped(idx):
    return np.tile(np.asarray(idx).reshape(-1, 16).T, (8, 1)).astype(np.uint16)


def unstriped(offs):
    return offs[:16].T.reshape(-1).astype(np.int64)


def striped8(idx):
    return np.asarray(idx).reshape(8, -1, 16).transpose(0, 2, 1).reshape(128, -1).astype(np.uint16)


def unstriped8(offs):
    return offs.reshape(8, 16, -1).transpose(0, 2, 1).reshape(8, -1).astype(np.int64)


def pick8(x, idx, run):
    r = np.arange(len(x))
    return x[r[:, None], idx[r % (8 * run) // run]]


E2M1 = np.array([0.0, 0.5, 1.0, 1.5, 2.0, 3.0, 4.0, 6.0, -0.0, -0.5, -1.0, -1.5, -2.0, -3.0, -4.0, -6.0])


def pack_weight(w, fmt):
    k, n = w.shape
    w = f64(np.asarray(w, np.float32).astype(ml_dtypes.bfloat16)).reshape(k // 32, 32, n)
    amax = np.abs(w).max(1)
    if fmt == "e4m3":
        byte = np.frexp(amax)[1] - 1 + 127 - 7
    else:
        mant, ex = np.frexp(amax / 6.0)
        byte = np.where(mant > 0.5, ex, ex - 1) + 127
    byte = np.clip(np.where(amax > 0, byte, 1), 1, 254)
    scaled = (w * np.exp2(127.0 - byte)[:, None, :]).reshape(k, n).astype(np.float32)
    by_word = np.ascontiguousarray(scaled.reshape(k // 512, 128, 4, n).transpose(0, 1, 3, 2))
    if fmt == "e4m3":
        words = by_word.astype(ml_dtypes.float8_e4m3fn).view(np.uint8)
    else:
        c = by_word.astype(ml_dtypes.float4_e2m1fn).view(np.uint8) & 0xF
        words = (c[..., 0::2] | (c[..., 1::2] << 4)).reshape(k // 512, 128, 2 * n)
    return np.ascontiguousarray(words), np.ascontiguousarray(byte.astype(np.uint8).reshape(k // 512, 16, n))


def unpack_weight(words, scales, fmt):
    g, _, n = scales.shape
    words = np.ascontiguousarray(words).reshape(g, 128, n, -1)
    if fmt == "e4m3":
        vals = words.view(ml_dtypes.float8_e4m3fn).astype(np.float64)
    else:
        nib = np.empty((g, 128, n, 4), np.uint8)
        nib[..., 0::2] = words & 0xF
        nib[..., 1::2] = words >> 4
        vals = E2M1[nib]
    vals = vals * np.repeat(np.exp2(scales.astype(np.float64) - 127.0), 8, axis=1)[..., None]
    return vals.transpose(0, 1, 3, 2).reshape(g * 512, n)


def sgn(shape):
    return np.random.uniform(0.5, 2.0, shape) * np.where(np.random.standard_normal(shape) < 0, -1.0, 1.0)


K, J, R, T, U, Z, M, O, N, E, G = 512, 512, 512, 2048, 2048, 512, 1024, 256, 256, 128, 512


def setup_inputs():
    n = np.random.standard_normal
    idx = np.stack([np.random.permutation(T)[:J] for _ in range(8)])
    idx2 = np.stack([np.random.permutation(U)[:J] for _ in range(8)])
    idx3 = np.random.permutation(M)[:J]
    idx4 = np.stack([np.random.permutation(J)[:O] for _ in range(8)])
    idx5 = np.stack([np.random.permutation(O)[:E] for _ in range(8)])
    idx6 = np.stack([np.random.permutation(G)[:E] for _ in range(8)])
    fk = mx_kscale(K)
    fr = mx_kscale(R)
    fz = mx_kscale(Z)
    wp = pack_weight(n((K, R)) * 1 / np.sqrt(K) / fk[:, None] * fr, "e4m3")
    xop = pack_weight(n((Z, M)) / fz[:, None], "e4m3")
    w2p = pack_weight(n((Z, R)) * 1 / np.sqrt(Z) * fz[:, None] * fr, "e2m1")
    wbp = pack_weight(n((R, N)) * 1 / np.sqrt(R) / fr[:, None], "e2m1")
    return {
        "ta": (np.random.randint(-7, 8, (K, T)).astype(np.float64)).astype(np.float32),
        "tb": (np.random.randint(1, 9, (K, U)).astype(np.float64)).astype(np.float32),
        "ga": ((np.random.randint(8, 25, (K, 1)) / 64.0) * fk[:, None]).astype(np.float32),
        "gb": (np.random.uniform(0.1, 0.4, (K, 1))).astype(np.float32),
        "w_words": wp[0],
        "w_scales": wp[1],
        "xo_words": xop[0],
        "xo_scales": xop[1],
        "w2_words": w2p[0],
        "w2_scales": w2p[1],
        "sa": (np.random.uniform(0.5, 1.6, (R, 1))).astype(np.float32),
        "wb_words": wbp[0],
        "wb_scales": wbp[1],
        "so": (sgn((N, 1))).astype(np.float32),
        "offs": striped8(idx),
        "offs2": striped8(idx2),
        "offs3": striped(idx3),
        "offs4": striped8(idx4),
        "offs5": striped8(idx5),
        "offs6": striped8(idx6),
    }


def reference(ta, tb, ga, gb, w_words, w_scales, xo_words, xo_scales, w2_words, w2_scales, sa, wb_words, wb_scales, so, offs, offs2, offs3, offs4, offs5, offs6):
    idx = unstriped8(offs)
    idx2 = unstriped8(offs2)
    idx3 = unstriped(offs3)
    idx4 = unstriped8(offs4)
    idx5 = unstriped8(offs5)
    idx6 = unstriped8(offs6)
    wu = unpack_weight(w_words, w_scales, "e4m3")
    xou = unpack_weight(xo_words, xo_scales, "e4m3")
    w2u = unpack_weight(w2_words, w2_scales, "e2m1")
    wbu = unpack_weight(wb_words, wb_scales, "e2m1")
    xc = pick8(f64(ta), idx, 64) * f64(ga) * pick8(f64(tb), idx2, 64) * f64(gb)
    xcq = mxq(xc, 0, "e4m3")
    xoidx3g = xou[:, idx3]
    a = wu.T @ xcq + w2u.T @ xoidx3g
    g1 = np.maximum(a, 0.0)
    hid = pick8(g1, idx4, 64) * f64(sa)
    hidq = mxq(hid, 0, "e4m3")
    p = wbu.T @ hidq
    m0 = pick8(p, idx5, 16) * f64(so)
    y = np.zeros((N, G))
    y[np.arange(N)[:, None], idx6[np.arange(N) % 128 // 16]] = m0
    return y

@@ -1,0 +1,218 @@
+from contextlib import ExitStack
+
+import concourse.mybir as mybir
+
+F32 = mybir.dt.float32
+BF16 = mybir.dt.bfloat16
+I32 = mybir.dt.int32
+U32 = mybir.dt.uint32
+U16 = mybir.dt.uint16
+U8 = mybir.dt.uint8
+FP8X4 = mybir.dt.float8_e4m3fn_x4
+FP4X4 = mybir.dt.float4_e2m1fn_x4
+ACT = mybir.ActivationFunctionType
+ALU = mybir.AluOpType
+
+P = 128
+PACK = 4
+K, J, R, T, Z, M, O, N, E, G = 512, 512, 512, 2048, 512, 1024, 256, 256, 128, 512
+JH = J // 2
+OH = O // 2
+QUADS = 4
+QUAD = 32
+FLOPS = 2 * (K * R * J + Z * R * J + R * N * O)
+
+
+def tile_picked_codegain_plain_bank_kept_one_posted_kernel(
+    tc, ta, tb, ga, gb, w_words, w_scales, xo_words, xo_scales, w2_words, w2_scales, sa,
+    wb_words, wb_scales, so, offs, offs2, offs3, offs4, offs5, offs6, out,
+):
+    nc = tc.nc
+    with ExitStack() as ctx:
+        keep = ctx.enter_context(tc.tile_pool(name="keep", bufs=1))
+        psum = ctx.enter_context(tc.psum_pool(name="psum", bufs=1))
+
+        def sb(name, shape, dtype):
+            return keep.tile(shape, dtype, name=name, align_bytes=64)
+
+        def load_list(name, src):
+            tile = keep.tile(list(src.shape), U16, name=name)
+            nc.sync.dma_start(tile[:], src)
+            return tile
+
+        def load_rows(name, table, t):
+            tile = sb(name, [P, T], F32)
+            nc.sync.dma_start(tile[:], table.rearrange("(p t) c -> t p c", t=PACK)[t])
+            return tile
+
+        def load_bytes(name, src, dtype, cols):
+            tile = sb(name, [P, cols], dtype)
+            nc.sync.dma_start(tile[:].bitcast(I32), src.bitcast(I32))
+            return tile
+
+        def load_dealt(name, vec):
+            tile = sb(name, [P, PACK], F32)
+            nc.gpsimd.dma_start(tile[:], vec.rearrange("(p t) o -> p (t o)", t=PACK))
+            return tile
+
+        def load_scales(name, scales, first):
+            cols = scales.shape[2]
+            staged = sb(name + "_staged", [P, QUADS, cols // 4], I32)
+            plane = sb(name + "_plane", [P, cols], U8)
+            nc.gpsimd.memset(staged[first : first + QUAD], 0)
+            nc.gpsimd.dma_start(
+                staged[first : first + 4], scales[0].bitcast(I32).rearrange("(q i) w -> i q w", i=4)
+            )
+            for q in range(QUADS):
+                nc.vector.tensor_copy(
+                    plane[QUAD * q : QUAD * (q + 1), :].bitcast(I32), staged[first : first + QUAD, q, :]
+                )
+            return plane
+
+        ga_t = load_dealt("ga_t", ga)
+        gb_t = load_dealt("gb_t", gb)
+        xo_plane = load_scales("xo", xo_scales, 0)
+        w2_plane = load_scales("w2", w2_scales, 64)
+        w_plane = load_scales("w", w_scales, 64)
+        wb_plane = load_scales("wb", wb_scales, 64)
+        sa_t = load_dealt("sa_t", sa)
+        so_t = sb("so_t", [P, N // P], F32)
+        with nc.allow_non_contiguous_dma(reason="one value a partition"):
+            nc.gpsimd.dma_start(so_t[:], so.rearrange("(b p) o -> p (b o)", p=P))
+
+        ta_t, tb_t = [], []
+        ta_t.append(load_rows("ta0", ta, 0))
+        list_a = load_list("list_a", offs)
+        list_b = load_list("list_b", offs2)
+        tb_t.append(load_rows("tb0", tb, 0))
+        list_xo = load_list("list_xo", offs3)
+        xo_raw = load_bytes("xo_raw", xo_words[0].rearrange("p n t -> p (n t)"), U32, M)
+        for t in (1, 2):
+            ta_t.append(load_rows("ta%d" % t, ta, t))
+            tb_t.append(load_rows("tb%d" % t, tb, t))
+        ta_t.append(load_rows("ta3", ta, 3))
+        w2_raw = load_bytes("w2_raw", w2_words[0], U8, 2 * R)
+        tb_t.append(load_rows("tb3", tb, 3))
+        w_raw = load_bytes("w_raw", w_words[0].rearrange("p n t -> p (n t)"), U32, R)
+        list_hid = load_list("list_hid", offs4)
+        wb_t = load_bytes("wb_t", wb_words[0], U8, 2 * N)
+        list_p = load_list("list_p", offs5)
+        list_out = load_list("list_out", offs6)
+
+        def deal(engine_copy, dst, src):
+            engine_copy(dst.rearrange("p (t m) -> p m t", t=PACK), src.rearrange("p (m t) -> p m t", t=PACK))
+
+        pages = [sb("page%d" % b, [P, G], F32) for b in range(N // P)]
+        for page in pages:
+            nc.vector.memset(page[:], 0.0)
+
+        w2_sc = sb("w2_sc", [P, R], U8)
+        deal(nc.vector.tensor_copy, w2_sc[:], w2_plane[:])
+        w_sc = sb("w_sc", [P, R], U8)
+        deal(nc.vector.tensor_copy, w_sc[:], w_plane[:])
+
+        xo_g = sb("xo_g", [P, J], U32)
+        xo_sc = sb("xo_sc", [P, J], U8)
+        nc.vector.tensor_copy(xo_sc[:], xo_plane[:].indirect(list_xo[:]))
+        nc.vector.tensor_copy(xo_g[:], xo_raw[:].indirect(list_xo[:]))
+
+        xc = [sb("xc%d" % h, [P, JH, PACK], BF16) for h in range(2)]
+        w2_d = sb("w2_d", [P, 2 * R], U8)
+        w_d = sb("w_d", [P, R], U32)
+        last = PACK - 1
+        for t in range(PACK):
+            code = sb("code%d" % t, [P, J], F32)
+            gain = sb("gain%d" % t, [P, J], F32)
+            nc.scalar.activation(code[:], ta_t[t][:].indirect(list_a[:]), ACT.Copy, scale=ga_t[:, t : t + 1])
+            if t == last:
+                deal(nc.scalar.copy, w2_d[:].bitcast(U16), w2_raw[:].bitcast(U16))
+                deal(nc.vector.tensor_copy, w_d[:], w_raw[:])
+            nc.scalar.activation(gain[:], tb_t[t][:].indirect(list_b[:]), ACT.Copy, scale=gb_t[:, t : t + 1])
+            if t < last:
+                for h in range(2):
+                    cols = slice(h * JH, (h + 1) * JH)
+                    nc.vector.tensor_tensor(xc[h][:, :, t], code[:, cols], gain[:, cols], ALU.mult)
+            else:
+                flat = sb("flat", [P, JH], BF16)
+                nc.vector.tensor_tensor(flat[:], code[:, :JH], gain[:, :JH], ALU.mult)
+                nc.scalar.copy(xc[0][:, :, t], flat[:])
+                nc.vector.tensor_tensor(xc[1][:, :, t], code[:, JH:], gain[:, JH:], ALU.mult)
+
+        xc_q = sb("xc_q", [P, J], U32)
+        xc_sc = sb("xc_sc", [P, J], U8)
+
+        banks = [[psum.tile([P, JH], F32, name="a0_%d" % h, tag="bank%d" % h) for h in range(2)]]
+        spans = [[slice(0, JH), slice(JH, J)]]
+        for t in range(1, PACK):
+            banks.append([psum.tile([P, J], F32, name="a%d" % t, tag="bank%d" % (t + 1))])
+            spans.append([slice(0, J)])
+        for t in range(PACK):
+            for bank, cols in zip(banks[t], spans[t]):
+                nc.tensor.matmul_mx(
+                    bank[:],
+                    lhsT=w2_d[:, 2 * P * t : 2 * P * (t + 1)].bitcast(FP4X4),
+                    lhsT_scale=w2_sc[:, P * t : P * (t + 1)],
+                    rhs=xo_g[:, cols].bitcast(FP8X4),
+                    rhs_scale=xo_sc[:, cols],
+                    start=True,
+                    stop=False,
+                )
+        for h in range(2):
+            cols = slice(h * JH, (h + 1) * JH)
+            nc.vector.quantize_mx(
+                xc_q[:, cols].bitcast(FP8X4), xc_sc[:, cols], xc[h][:].rearrange("p j t -> p (j t)")
+            )
+        g1 = [sb("g1_%d" % t, [P, J], F32) for t in range(PACK)]
+        for t in range(PACK):
+            for bank, cols in zip(banks[t], spans[t]):
+                nc.tensor.matmul_mx(
+                    bank[:],
+                    lhsT=w_d[:, P * t : P * (t + 1)].bitcast(FP8X4),
+                    lhsT_scale=w_sc[:, P * t : P * (t + 1)],
+                    rhs=xc_q[:, cols].bitcast(FP8X4),
+                    rhs_scale=xc_sc[:, cols],
+                    start=False,
+                    stop=True,
+                )
+                if t == 0 and cols.start == 0:
+                    nc.scalar.activation(g1[t][:, cols], bank[:], ACT.Relu)
+                else:
+                    nc.vector.tensor_scalar_max(g1[t][:, cols], bank[:], 0.0)
+
+        p_t = [sb("p%d" % b, [P, O], F32) for b in range(N // P)]
+        for h in range(2):
+            hid = sb("hid%d" % h, [P, PACK, OH], BF16)
+            lcols = slice(h * OH // 16, (h + 1) * OH // 16)
+            for t in range(PACK):
+                nc.scalar.activation(
+                    hid[:, t, :], g1[t][:].indirect(list_hid[:, lcols]), ACT.Copy, scale=sa_t[:, t : t + 1]
+                )
+            woven = sb("woven%d" % h, [P, OH, PACK], BF16)
+            nc.vector.tensor_copy(
+                woven[:].rearrange("p (c i) t -> p c t i", i=4), hid[:].rearrange("p t (c i) -> p c t i", i=4)
+            )
+            hid_q = sb("hid_q%d" % h, [P, OH], U32)
+            hid_sc = sb("hid_sc%d" % h, [P, OH], U8)
+            nc.vector.quantize_mx(hid_q[:].bitcast(FP8X4), hid_sc[:], woven[:].rearrange("p o t -> p (o t)"))
+            for b in range(N // P):
+                bank = psum.tile([P, OH], F32, name="pp%d_%d" % (h, b), tag="bank%d" % ((5 + 2 * h + b) % 8))
+                nc.tensor.matmul_mx(
+                    bank[:],
+                    lhsT=wb_t[:, 2 * P * b : 2 * P * (b + 1)].bitcast(FP4X4),
+                    lhsT_scale=wb_plane[:, P * b : P * (b + 1)],
+                    rhs=hid_q[:].bitcast(FP8X4),
+                    rhs_scale=hid_sc[:],
+                    start=True,
+                    stop=True,
+                )
+                dst = p_t[b][:, h * OH : (h + 1) * OH]
+                if h == 1 and b == 1:
+                    nc.vector.tensor_copy(dst, bank[:])
+                else:
+                    nc.scalar.activation(dst, bank[:], ACT.Copy)
+
+        for b in range(N // P):
+            ends = sb("ends%d" % b, [P, E], F32)
+            nc.scalar.activation(ends[:], p_t[b][:].indirect(list_p[:]), ACT.Copy, scale=so_t[:, b : b + 1])
+            nc.vector.tensor_copy(pages[b][:].indirect(list_out[:]), ends[:])
+            nc.sync.dma_start(out[P * b : P * (b + 1), :], pages[b][:])

@@ -52,15 +52,15 @@ def tile_picked_codegain_plain_bank_kept_one_posted_kernel(
 
         def load_dealt(name, vec):
             tile = sb(name, [P, PACK], F32)
-            nc.gpsimd.dma_start(tile[:], vec.rearrange("(p t) o -> p (t o)", t=PACK))
+            nc.sync.dma_start(tile[:], vec.rearrange("(p t) o -> p (t o)", t=PACK))
             return tile
 
         def load_scales(name, scales, first):
             cols = scales.shape[2]
             staged = sb(name + "_staged", [P, QUADS, cols // 4], I32)
             plane = sb(name + "_plane", [P, cols], U8)
-            nc.gpsimd.memset(staged[first : first + QUAD], 0)
-            nc.gpsimd.dma_start(
+            nc.vector.memset(staged[first : first + QUAD], 0)
+            nc.sync.dma_start(
                 staged[first : first + 4], scales[0].bitcast(I32).rearrange("(q i) w -> i q w", i=4)
             )
             for q in range(QUADS):
@@ -69,34 +69,39 @@ def tile_picked_codegain_plain_bank_kept_one_posted_kernel(
                 )
             return plane
 
-        ga_t = load_dealt("ga_t", ga)
-        gb_t = load_dealt("gb_t", gb)
-        xo_plane = load_scales("xo", xo_scales, 0)
-        w2_plane = load_scales("w2", w2_scales, 64)
-        w_plane = load_scales("w", w_scales, 64)
-        wb_plane = load_scales("wb", wb_scales, 64)
-        sa_t = load_dealt("sa_t", sa)
-        so_t = sb("so_t", [P, N // P], F32)
-        with nc.allow_non_contiguous_dma(reason="one value a partition"):
-            nc.gpsimd.dma_start(so_t[:], so.rearrange("(b p) o -> p (b o)", p=P))
-
         ta_t, tb_t = [], []
         ta_t.append(load_rows("ta0", ta, 0))
         list_a = load_list("list_a", offs)
-        list_b = load_list("list_b", offs2)
-        tb_t.append(load_rows("tb0", tb, 0))
+        ga_t = load_dealt("ga_t", ga)
         list_xo = load_list("list_xo", offs3)
-        xo_raw = load_bytes("xo_raw", xo_words[0].rearrange("p n t -> p (n t)"), U32, M)
-        for t in (1, 2):
-            ta_t.append(load_rows("ta%d" % t, ta, t))
-            tb_t.append(load_rows("tb%d" % t, tb, t))
-        ta_t.append(load_rows("ta3", ta, 3))
+        tb_t.append(load_rows("tb0", tb, 0))
+        list_b = load_list("list_b", offs2)
+        gb_t = load_dealt("gb_t", gb)
         w2_raw = load_bytes("w2_raw", w2_words[0], U8, 2 * R)
+        ta_t.append(load_rows("ta1", ta, 1))
+        xo_plane = load_scales("xo", xo_scales, 0)
+        w2_plane = load_scales("w2", w2_scales, 64)
+        w_plane = load_scales("w", w_scales, 64)
+        tb_t.append(load_rows("tb1", tb, 1))
+        ta_t.append(load_rows("ta2", ta, 2))
+        tb_t.append(load_rows("tb2", tb, 2))
+        ta_t.append(load_rows("ta3", ta, 3))
+        xo_raw = load_bytes("xo_raw", xo_words[0].rearrange("p n t -> p (n t)"), U32, M)
         tb_t.append(load_rows("tb3", tb, 3))
         w_raw = load_bytes("w_raw", w_words[0].rearrange("p n t -> p (n t)"), U32, R)
         list_hid = load_list("list_hid", offs4)
+        sa_t = load_dealt("sa_t", sa)
         wb_t = load_bytes("wb_t", wb_words[0], U8, 2 * N)
+        wb_plane = sb("wb_plane", [P, N], U8)
+        nc.vector.memset(wb_plane[:].bitcast(I32), 0)
+        for q in range(QUADS):
+            nc.sync.dma_start(
+                wb_plane[QUAD * q : QUAD * q + 4, :].bitcast(I32), wb_scales[0, 4 * q : 4 * q + 4, :].bitcast(I32)
+            )
         list_p = load_list("list_p", offs5)
+        so_t = sb("so_t", [P, N // P], F32)
+        with nc.allow_non_contiguous_dma(reason="one value a partition"):
+            nc.sync.dma_start(so_t[:], so.rearrange("(b p) o -> p (b o)", p=P))
         list_out = load_list("list_out", offs6)
 
         def deal(engine_copy, dst, src):
@@ -114,18 +119,18 @@ def tile_picked_codegain_plain_bank_kept_one_posted_kernel(
         xo_g = sb("xo_g", [P, J], U32)
         xo_sc = sb("xo_sc", [P, J], U8)
         nc.vector.tensor_copy(xo_sc[:], xo_plane[:].indirect(list_xo[:]))
-        nc.vector.tensor_copy(xo_g[:], xo_raw[:].indirect(list_xo[:]))
 
         xc = [sb("xc%d" % h, [P, JH, PACK], BF16) for h in range(2)]
         w2_d = sb("w2_d", [P, 2 * R], U8)
         w_d = sb("w_d", [P, R], U32)
+        deal(nc.scalar.copy, w2_d[:].bitcast(U16), w2_raw[:].bitcast(U16))
         last = PACK - 1
         for t in range(PACK):
             code = sb("code%d" % t, [P, J], F32)
             gain = sb("gain%d" % t, [P, J], F32)
             nc.scalar.activation(code[:], ta_t[t][:].indirect(list_a[:]), ACT.Copy, scale=ga_t[:, t : t + 1])
             if t == last:
-                deal(nc.scalar.copy, w2_d[:].bitcast(U16), w2_raw[:].bitcast(U16))
+                nc.vector.tensor_copy(xo_g[:], xo_raw[:].indirect(list_xo[:]))
                 deal(nc.vector.tensor_copy, w_d[:], w_raw[:])
             nc.scalar.activation(gain[:], tb_t[t][:].indirect(list_b[:]), ACT.Copy, scale=gb_t[:, t : t + 1])
             if t < last:

@@ -55,49 +55,50 @@ def tile_picked_codegain_plain_bank_kept_one_posted_kernel(
             nc.sync.dma_start(tile[:], vec.rearrange("(p t) o -> p (t o)", t=PACK))
             return tile
 
-        def load_scales(name, scales, first):
-            cols = scales.shape[2]
-            staged = sb(name + "_staged", [P, QUADS, cols // 4], I32)
-            plane = sb(name + "_plane", [P, cols], U8)
-            nc.vector.memset(staged[first : first + QUAD], 0)
-            nc.sync.dma_start(
-                staged[first : first + 4], scales[0].bitcast(I32).rearrange("(q i) w -> i q w", i=4)
-            )
-            for q in range(QUADS):
-                nc.vector.tensor_copy(
-                    plane[QUAD * q : QUAD * (q + 1), :].bitcast(I32), staged[first : first + QUAD, q, :]
-                )
+        def scale_plane(name, scales):
+            plane = sb(name, [P, scales.shape[2]], U8)
+            nc.vector.memset(plane[:].bitcast(I32), 0)
             return plane
+
+        def load_scale_rows(plane, scales, i):
+            nc.sync.dma_start(
+                plane[i:P:QUAD, :].bitcast(I32), scales[0].bitcast(I32).rearrange("(q i) w -> i q w", i=4)[i]
+            )
+
+        xo_plane = scale_plane("xo_plane", xo_scales)
+        w2_plane = scale_plane("w2_plane", w2_scales)
+        w_plane = scale_plane("w_plane", w_scales)
+        wb_plane = scale_plane("wb_plane", wb_scales)
+        row_loads = [
+            (plane, scales, i)
+            for plane, scales in ((w2_plane, w2_scales), (w_plane, w_scales), (xo_plane, xo_scales))
+            for i in range(4)
+        ]
 
         ta_t, tb_t = [], []
         ta_t.append(load_rows("ta0", ta, 0))
         list_a = load_list("list_a", offs)
         ga_t = load_dealt("ga_t", ga)
-        list_xo = load_list("list_xo", offs3)
         tb_t.append(load_rows("tb0", tb, 0))
         list_b = load_list("list_b", offs2)
         gb_t = load_dealt("gb_t", gb)
         w2_raw = load_bytes("w2_raw", w2_words[0], U8, 2 * R)
-        ta_t.append(load_rows("ta1", ta, 1))
-        xo_plane = load_scales("xo", xo_scales, 0)
-        w2_plane = load_scales("w2", w2_scales, 64)
-        w_plane = load_scales("w", w_scales, 64)
-        tb_t.append(load_rows("tb1", tb, 1))
-        ta_t.append(load_rows("ta2", ta, 2))
-        tb_t.append(load_rows("tb2", tb, 2))
+        for t in (1, 2):
+            for half, (tiles, name, table) in enumerate(((ta_t, "ta", ta), (tb_t, "tb", tb))):
+                tiles.append(load_rows("%s%d" % (name, t), table, t))
+                first = 3 * (2 * (t - 1) + half)
+                for args in row_loads[first : first + 3]:
+                    load_scale_rows(*args)
         ta_t.append(load_rows("ta3", ta, 3))
         xo_raw = load_bytes("xo_raw", xo_words[0].rearrange("p n t -> p (n t)"), U32, M)
+        list_xo = load_list("list_xo", offs3)
         tb_t.append(load_rows("tb3", tb, 3))
         w_raw = load_bytes("w_raw", w_words[0].rearrange("p n t -> p (n t)"), U32, R)
         list_hid = load_list("list_hid", offs4)
         sa_t = load_dealt("sa_t", sa)
         wb_t = load_bytes("wb_t", wb_words[0], U8, 2 * N)
-        wb_plane = sb("wb_plane", [P, N], U8)
-        nc.vector.memset(wb_plane[:].bitcast(I32), 0)
-        for q in range(QUADS):
-            nc.sync.dma_start(
-                wb_plane[QUAD * q : QUAD * q + 4, :].bitcast(I32), wb_scales[0, 4 * q : 4 * q + 4, :].bitcast(I32)
-            )
+        for i in range(4):
+            load_scale_rows(wb_plane, wb_scales, i)
         list_p = load_list("list_p", offs5)
         so_t = sb("so_t", [P, N // P], F32)
         with nc.allow_non_contiguous_dma(reason="one value a partition"):
@@ -118,9 +119,9 @@ def tile_picked_codegain_plain_bank_kept_one_posted_kernel(
 
         xo_g = sb("xo_g", [P, J], U32)
         xo_sc = sb("xo_sc", [P, J], U8)
-        nc.vector.tensor_copy(xo_sc[:], xo_plane[:].indirect(list_xo[:]))
 
-        xc = [sb("xc%d" % h, [P, JH, PACK], BF16) for h in range(2)]
+        pieces = [slice(0, J // 2), slice(J // 2, 3 * J // 4), slice(3 * J // 4, J)]
+        xc = [sb("xc%d" % h, [P, cols.stop - cols.start, PACK], BF16) for h, cols in enumerate(pieces)]
         w2_d = sb("w2_d", [P, 2 * R], U8)
         w_d = sb("w_d", [P, R], U32)
         deal(nc.scalar.copy, w2_d[:].bitcast(U16), w2_raw[:].bitcast(U16))
@@ -131,25 +132,31 @@ def tile_picked_codegain_plain_bank_kept_one_posted_kernel(
             nc.scalar.activation(code[:], ta_t[t][:].indirect(list_a[:]), ACT.Copy, scale=ga_t[:, t : t + 1])
             if t == last:
                 nc.vector.tensor_copy(xo_g[:], xo_raw[:].indirect(list_xo[:]))
+                nc.vector.tensor_copy(xo_sc[:], xo_plane[:].indirect(list_xo[:]))
                 deal(nc.vector.tensor_copy, w_d[:], w_raw[:])
             nc.scalar.activation(gain[:], tb_t[t][:].indirect(list_b[:]), ACT.Copy, scale=gb_t[:, t : t + 1])
             if t < last:
-                for h in range(2):
-                    cols = slice(h * JH, (h + 1) * JH)
+                for h, cols in enumerate(pieces):
                     nc.vector.tensor_tensor(xc[h][:, :, t], code[:, cols], gain[:, cols], ALU.mult)
             else:
                 flat = sb("flat", [P, JH], BF16)
-                nc.vector.tensor_tensor(flat[:], code[:, :JH], gain[:, :JH], ALU.mult)
-                nc.scalar.copy(xc[0][:, :, t], flat[:])
-                nc.vector.tensor_tensor(xc[1][:, :, t], code[:, JH:], gain[:, JH:], ALU.mult)
+                nc.vector.tensor_tensor(flat[:], code[:, JH:], gain[:, JH:], ALU.mult)
+                for h in (1, 2):
+                    nc.scalar.copy(xc[h][:, :, t], flat[:, pieces[h].start - JH : pieces[h].stop - JH])
+                nc.vector.tensor_tensor(xc[0][:, :, t], code[:, :JH], gain[:, :JH], ALU.mult)
 
         xc_q = sb("xc_q", [P, J], U32)
         xc_sc = sb("xc_sc", [P, J], U8)
 
-        banks = [[psum.tile([P, JH], F32, name="a0_%d" % h, tag="bank%d" % h) for h in range(2)]]
-        spans = [[slice(0, JH), slice(JH, J)]]
+        banks = [
+            [
+                psum.tile([P, cols.stop - cols.start], F32, name="a0_%d" % h, tag="bank%d" % h)
+                for h, cols in enumerate(pieces)
+            ]
+        ]
+        spans = [pieces]
         for t in range(1, PACK):
-            banks.append([psum.tile([P, J], F32, name="a%d" % t, tag="bank%d" % (t + 1))])
+            banks.append([psum.tile([P, J], F32, name="a%d" % t, tag="bank%d" % (t + 2))])
             spans.append([slice(0, J)])
         for t in range(PACK):
             for bank, cols in zip(banks[t], spans[t]):
@@ -162,8 +169,7 @@ def tile_picked_codegain_plain_bank_kept_one_posted_kernel(
                     start=True,
                     stop=False,
                 )
-        for h in range(2):
-            cols = slice(h * JH, (h + 1) * JH)
+        for h, cols in enumerate(pieces):
             nc.vector.quantize_mx(
                 xc_q[:, cols].bitcast(FP8X4), xc_sc[:, cols], xc[h][:].rearrange("p j t -> p (j t)")
             )
@@ -179,28 +185,31 @@ def tile_picked_codegain_plain_bank_kept_one_posted_kernel(
                     start=False,
                     stop=True,
                 )
-                if t == 0 and cols.start == 0:
+                if t == 0:
                     nc.scalar.activation(g1[t][:, cols], bank[:], ACT.Relu)
                 else:
                     nc.vector.tensor_scalar_max(g1[t][:, cols], bank[:], 0.0)
 
         p_t = [sb("p%d" % b, [P, O], F32) for b in range(N // P)]
-        for h in range(2):
-            hid = sb("hid%d" % h, [P, PACK, OH], BF16)
-            lcols = slice(h * OH // 16, (h + 1) * OH // 16)
-            for t in range(PACK):
+        hid = sb("hid", [P, PACK, O], BF16)
+        for t in range(PACK):
+            for start, stop in [(0, O)] if t < last else [(0, OH), (OH, O)]:
                 nc.scalar.activation(
-                    hid[:, t, :], g1[t][:].indirect(list_hid[:, lcols]), ACT.Copy, scale=sa_t[:, t : t + 1]
+                    hid[:, t, start:stop],
+                    g1[t][:].indirect(list_hid[:, start // 16 : stop // 16]),
+                    ACT.Copy,
+                    scale=sa_t[:, t : t + 1],
                 )
+        for h in range(2):
             woven = sb("woven%d" % h, [P, OH, PACK], BF16)
             nc.vector.tensor_copy(
-                woven[:].rearrange("p (c i) t -> p c t i", i=4), hid[:].rearrange("p t (c i) -> p c t i", i=4)
+                woven[:].rearrange("p (c i) t -> p c t i", i=4), hid[:, :, h * OH : (h + 1) * OH].rearrange("p t (c i) -> p c t i", i=4)
             )
             hid_q = sb("hid_q%d" % h, [P, OH], U32)
             hid_sc = sb("hid_sc%d" % h, [P, OH], U8)
             nc.vector.quantize_mx(hid_q[:].bitcast(FP8X4), hid_sc[:], woven[:].rearrange("p o t -> p (o t)"))
             for b in range(N // P):
-                bank = psum.tile([P, OH], F32, name="pp%d_%d" % (h, b), tag="bank%d" % ((5 + 2 * h + b) % 8))
+                bank = psum.tile([P, OH], F32, name="pp%d_%d" % (h, b), tag="bank%d" % ((6 + 2 * h + b) % 8))
                 nc.tensor.matmul_mx(
                     bank[:],
                     lhsT=wb_t[:, 2 * P * b : 2 * P * (b + 1)].bitcast(FP4X4),

from contextlib import ExitStack

import concourse.mybir as mybir

F32 = mybir.dt.float32
BF16 = mybir.dt.bfloat16
I32 = mybir.dt.int32
U32 = mybir.dt.uint32
U16 = mybir.dt.uint16
U8 = mybir.dt.uint8
FP8X4 = mybir.dt.float8_e4m3fn_x4
FP4X4 = mybir.dt.float4_e2m1fn_x4
ACT = mybir.ActivationFunctionType
ALU = mybir.AluOpType

P = 128
PACK = 4
K, J, R, T, Z, M, O, N, E, G = 512, 512, 512, 2048, 512, 1024, 256, 256, 128, 512
JH = J // 2
OH = O // 2
QUADS = 4
QUAD = 32
FLOPS = 2 * (K * R * J + Z * R * J + R * N * O)


def tile_picked_codegain_plain_bank_kept_one_posted_kernel(
    tc, ta, tb, ga, gb, w_words, w_scales, xo_words, xo_scales, w2_words, w2_scales, sa,
    wb_words, wb_scales, so, offs, offs2, offs3, offs4, offs5, offs6, out,
):
    nc = tc.nc
    with ExitStack() as ctx:
        keep = ctx.enter_context(tc.tile_pool(name="keep", bufs=1))
        psum = ctx.enter_context(tc.psum_pool(name="psum", bufs=1))

        def sb(name, shape, dtype):
            return keep.tile(shape, dtype, name=name, align_bytes=64)

        def load_list(name, src):
            tile = keep.tile(list(src.shape), U16, name=name)
            nc.sync.dma_start(tile[:], src)
            return tile

        def load_rows(name, table, t):
            tile = sb(name, [P, T], F32)
            nc.sync.dma_start(tile[:], table.rearrange("(p t) c -> t p c", t=PACK)[t])
            return tile

        def load_bytes(name, src, dtype, cols):
            tile = sb(name, [P, cols], dtype)
            nc.sync.dma_start(tile[:].bitcast(I32), src.bitcast(I32))
            return tile

        def load_dealt(name, vec):
            tile = sb(name, [P, PACK], F32)
            nc.sync.dma_start(tile[:], vec.rearrange("(p t) o -> p (t o)", t=PACK))
            return tile

        def scale_plane(name, scales):
            plane = sb(name, [P, scales.shape[2]], U8)
            nc.vector.memset(plane[:].bitcast(I32), 0)
            return plane

        def load_scale_rows(plane, scales, i):
            nc.sync.dma_start(
                plane[i:P:QUAD, :].bitcast(I32), scales[0].bitcast(I32).rearrange("(q i) w -> i q w", i=4)[i]
            )

        xo_plane = scale_plane("xo_plane", xo_scales)
        w2_plane = scale_plane("w2_plane", w2_scales)
        w_plane = scale_plane("w_plane", w_scales)
        wb_plane = scale_plane("wb_plane", wb_scales)
        row_loads = [
            (plane, scales, i)
            for plane, scales in ((w2_plane, w2_scales), (w_plane, w_scales), (xo_plane, xo_scales))
            for i in range(4)
        ]

        ta_t, tb_t = [], []
        ta_t.append(load_rows("ta0", ta, 0))
        list_a = load_list("list_a", offs)
        ga_t = load_dealt("ga_t", ga)
        tb_t.append(load_rows("tb0", tb, 0))
        list_b = load_list("list_b", offs2)
        gb_t = load_dealt("gb_t", gb)
        w2_raw = load_bytes("w2_raw", w2_words[0], U8, 2 * R)
        for t in (1, 2):
            for half, (tiles, name, table) in enumerate(((ta_t, "ta", ta), (tb_t, "tb", tb))):
                tiles.append(load_rows("%s%d" % (name, t), table, t))
                first = 3 * (2 * (t - 1) + half)
                for args in row_loads[first : first + 3]:
                    load_scale_rows(*args)
        ta_t.append(load_rows("ta3", ta, 3))
        xo_raw = load_bytes("xo_raw", xo_words[0].rearrange("p n t -> p (n t)"), U32, M)
        list_xo = load_list("list_xo", offs3)
        tb_t.append(load_rows("tb3", tb, 3))
        w_raw = load_bytes("w_raw", w_words[0].rearrange("p n t -> p (n t)"), U32, R)
        list_hid = load_list("list_hid", offs4)
        sa_t = load_dealt("sa_t", sa)
        wb_t = load_bytes("wb_t", wb_words[0], U8, 2 * N)
        for i in range(4):
            load_scale_rows(wb_plane, wb_scales, i)
        list_p = load_list("list_p", offs5)
        so_t = sb("so_t", [P, N // P], F32)
        with nc.allow_non_contiguous_dma(reason="one value a partition"):
            nc.sync.dma_start(so_t[:], so.rearrange("(b p) o -> p (b o)", p=P))
        list_out = load_list("list_out", offs6)

        def deal(engine_copy, dst, src):
            engine_copy(dst.rearrange("p (t m) -> p m t", t=PACK), src.rearrange("p (m t) -> p m t", t=PACK))

        pages = [sb("page%d" % b, [P, G], F32) for b in range(N // P)]
        for page in pages:
            nc.vector.memset(page[:], 0.0)

        w2_sc = sb("w2_sc", [P, R], U8)
        deal(nc.vector.tensor_copy, w2_sc[:], w2_plane[:])
        w_sc = sb("w_sc", [P, R], U8)
        deal(nc.vector.tensor_copy, w_sc[:], w_plane[:])

        xo_g = sb("xo_g", [P, J], U32)
        xo_sc = sb("xo_sc", [P, J], U8)

        pieces = [slice(0, J // 2), slice(J // 2, 3 * J // 4), slice(3 * J // 4, J)]
        xc = [sb("xc%d" % h, [P, cols.stop - cols.start, PACK], BF16) for h, cols in enumerate(pieces)]
        w2_d = sb("w2_d", [P, 2 * R], U8)
        w_d = sb("w_d", [P, R], U32)
        deal(nc.scalar.copy, w2_d[:].bitcast(U16), w2_raw[:].bitcast(U16))
        last = PACK - 1
        for t in range(PACK):
            code = sb("code%d" % t, [P, J], F32)
            gain = sb("gain%d" % t, [P, J], F32)
            nc.scalar.activation(code[:], ta_t[t][:].indirect(list_a[:]), ACT.Copy, scale=ga_t[:, t : t + 1])
            if t == last:
                nc.vector.tensor_copy(xo_g[:], xo_raw[:].indirect(list_xo[:]))
                nc.vector.tensor_copy(xo_sc[:], xo_plane[:].indirect(list_xo[:]))
                deal(nc.vector.tensor_copy, w_d[:], w_raw[:])
            nc.scalar.activation(gain[:], tb_t[t][:].indirect(list_b[:]), ACT.Copy, scale=gb_t[:, t : t + 1])
            if t < last:
                for h, cols in enumerate(pieces):
                    nc.vector.tensor_tensor(xc[h][:, :, t], code[:, cols], gain[:, cols], ALU.mult)
            else:
                flat = sb("flat", [P, JH], BF16)
                nc.vector.tensor_tensor(flat[:], code[:, JH:], gain[:, JH:], ALU.mult)
                for h in (1, 2):
                    nc.scalar.copy(xc[h][:, :, t], flat[:, pieces[h].start - JH : pieces[h].stop - JH])
                nc.vector.tensor_tensor(xc[0][:, :, t], code[:, :JH], gain[:, :JH], ALU.mult)

        xc_q = sb("xc_q", [P, J], U32)
        xc_sc = sb("xc_sc", [P, J], U8)

        banks = [
            [
                psum.tile([P, cols.stop - cols.start], F32, name="a0_%d" % h, tag="bank%d" % h)
                for h, cols in enumerate(pieces)
            ]
        ]
        spans = [pieces]
        for t in range(1, PACK):
            banks.append([psum.tile([P, J], F32, name="a%d" % t, tag="bank%d" % (t + 2))])
            spans.append([slice(0, J)])
        for t in range(PACK):
            for bank, cols in zip(banks[t], spans[t]):
                nc.tensor.matmul_mx(
                    bank[:],
                    lhsT=w2_d[:, 2 * P * t : 2 * P * (t + 1)].bitcast(FP4X4),
                    lhsT_scale=w2_sc[:, P * t : P * (t + 1)],
                    rhs=xo_g[:, cols].bitcast(FP8X4),
                    rhs_scale=xo_sc[:, cols],
                    start=True,
                    stop=False,
                )
        for h, cols in enumerate(pieces):
            nc.vector.quantize_mx(
                xc_q[:, cols].bitcast(FP8X4), xc_sc[:, cols], xc[h][:].rearrange("p j t -> p (j t)")
            )
        g1 = [sb("g1_%d" % t, [P, J], F32) for t in range(PACK)]
        for t in range(PACK):
            for bank, cols in zip(banks[t], spans[t]):
                nc.tensor.matmul_mx(
                    bank[:],
                    lhsT=w_d[:, P * t : P * (t + 1)].bitcast(FP8X4),
                    lhsT_scale=w_sc[:, P * t : P * (t + 1)],
                    rhs=xc_q[:, cols].bitcast(FP8X4),
                    rhs_scale=xc_sc[:, cols],
                    start=False,
                    stop=True,
                )
                if t == 0:
                    nc.scalar.activation(g1[t][:, cols], bank[:], ACT.Relu)
                else:
                    nc.vector.tensor_scalar_max(g1[t][:, cols], bank[:], 0.0)

        p_t = [sb("p%d" % b, [P, O], F32) for b in range(N // P)]
        hid = sb("hid", [P, PACK, O], BF16)
        for t in range(PACK):
            for start, stop in [(0, O)] if t < last else [(0, OH), (OH, O)]:
                nc.scalar.activation(
                    hid[:, t, start:stop],
                    g1[t][:].indirect(list_hid[:, start // 16 : stop // 16]),
                    ACT.Copy,
                    scale=sa_t[:, t : t + 1],
                )
        for h in range(2):
            woven = sb("woven%d" % h, [P, OH, PACK], BF16)
            nc.vector.tensor_copy(
                woven[:].rearrange("p (c i) t -> p c t i", i=4), hid[:, :, h * OH : (h + 1) * OH].rearrange("p t (c i) -> p c t i", i=4)
            )
            hid_q = sb("hid_q%d" % h, [P, OH], U32)
            hid_sc = sb("hid_sc%d" % h, [P, OH], U8)
            nc.vector.quantize_mx(hid_q[:].bitcast(FP8X4), hid_sc[:], woven[:].rearrange("p o t -> p (o t)"))
            for b in range(N // P):
                bank = psum.tile([P, OH], F32, name="pp%d_%d" % (h, b), tag="bank%d" % ((6 + 2 * h + b) % 8))
                nc.tensor.matmul_mx(
                    bank[:],
                    lhsT=wb_t[:, 2 * P * b : 2 * P * (b + 1)].bitcast(FP4X4),
                    lhsT_scale=wb_plane[:, P * b : P * (b + 1)],
                    rhs=hid_q[:].bitcast(FP8X4),
                    rhs_scale=hid_sc[:],
                    start=True,
                    stop=True,
                )
                dst = p_t[b][:, h * OH : (h + 1) * OH]
                if h == 1 and b == 1:
                    nc.vector.tensor_copy(dst, bank[:])
                else:
                    nc.scalar.activation(dst, bank[:], ACT.Copy)

        for b in range(N // P):
            ends = sb("ends%d" % b, [P, E], F32)
            nc.scalar.activation(ends[:], p_t[b][:].indirect(list_p[:]), ACT.Copy, scale=so_t[:, b : b + 1])
            nc.vector.tensor_copy(pages[b][:].indirect(list_out[:]), ends[:])
            nc.sync.dma_start(out[P * b : P * (b + 1), :], pages[b][:])
